import numpy as np
import ml_dtypes


def mxq(x, axis, fmt="e4m3"):
    dtype, down = {"e4m3": (ml_dtypes.float8_e4m3fn, 7), "e5m2": (ml_dtypes.float8_e5m2, 14)}[fmt]
    v = np.moveaxis(np.asarray(x, np.float32).astype(ml_dtypes.bfloat16).astype(np.float64), axis, -1)
    blocks = v.reshape(v.shape[:-1] + (-1, 32))
    amax = np.abs(blocks).max(-1, keepdims=True)
    byte = np.maximum(np.where(amax > 0, np.frexp(amax)[1] - 1 + 127, 0) - down, 1)
    scale = np.exp2(byte - 127.0)
    codes = (blocks / scale).astype(np.float32).astype(dtype).astype(np.float64)
    return np.moveaxis((codes * scale).reshape(v.shape), -1, axis)


WIDE = False


def mx_kscale(k):
    if not WIDE:
        return np.ones(k)
    levels = np.array([10, -10, 5, -5, 0])
    if k % 512:
        return np.exp2(np.random.permutation(np.resize(levels, k // 32))).repeat(32)
    a = np.empty((k // 512, 16))
    for p in range(k // 512):
        a[p, :8] = np.random.permutation(np.resize(levels, 8))
        for g in range(8):
            far = levels[np.abs(levels - a[p, g]) >= 10]
            a[p, g + 8] = far[np.random.randint(len(far))]
    return np.exp2(a.ravel()).repeat(32)


BF16 = ml_dtypes.bfloat16


def bf(x):
    return np.asarray(x, np.float32).astype(BF16)


def f64(x):
    return np.asarray(x).astype(np.float64)


E2M1 = np.array([0.0, 0.5, 1.0, 1.5, 2.0, 3.0, 4.0, 6.0, -0.0, -0.5, -1.0, -1.5, -2.0, -3.0, -4.0, -6.0])


def pack_weight(w, fmt):
    k, n = w.shape
    w = f64(bf(w)).reshape(k // 32, 32, n)
    amax = np.abs(w).max(1)
    if fmt == "e4m3":
        byte = np.frexp(amax)[1] - 1 + 127 - 7
    else:
        mant, ex = np.frexp(amax / 6.0)
        byte = np.where(mant > 0.5, ex, ex - 1) + 127
    byte = np.clip(np.where(amax > 0, byte, 1), 1, 254)
    scaled = (w * np.exp2(127.0 - byte)[:, None, :]).reshape(k, n).astype(np.float32)
    by_word = np.ascontiguousarray(scaled.reshape(k // 512, 128, 4, n).transpose(0, 1, 3, 2))
    if fmt == "e4m3":
        words = by_word.astype(ml_dtypes.float8_e4m3fn).view(np.uint8)
    else:
        c = by_word.astype(ml_dtypes.float4_e2m1fn).view(np.uint8) & 0xF
        words = c[..., 0::2] | (c[..., 1::2] << 4)
    return np.ascontiguousarray(words), np.ascontiguousarray(byte.astype(np.uint8).reshape(k // 512, 16, n))


def unpack_weight(words, scales, fmt):
    g, p, n, _ = words.shape
    if fmt == "e4m3":
        vals = np.ascontiguousarray(words).view(ml_dtypes.float8_e4m3fn).astype(np.float64)
    else:
        nib = np.empty((g, p, n, 4), np.uint8)
        nib[..., 0::2] = words & 0xF
        nib[..., 1::2] = words >> 4
        vals = E2M1[nib]
    vals = vals * np.repeat(np.exp2(scales.astype(np.float64) - 127.0), 8, axis=1)[..., None]
    return vals.transpose(0, 1, 3, 2).reshape(g * 512, n)
def pack4(w):
    words, scales = pack_weight(w, "e2m1")
    return words.reshape(words.shape[0], 128, -1), scales


def unpack4(words, scales):
    return unpack_weight(words.reshape(words.shape[0], 128, -1, 2), scales, "e2m1")


B, T, K, D, L = 1024, 1024, 1024, 512, 8


def setup_inputs():
    s, t = mx_kscale(K), mx_kscale(T)
    terms = np.random.standard_normal((K, T)) / np.sqrt(K) * s[:, None] * t
    docs = np.random.standard_normal((K, D * L)) / s[:, None]
    terms_words, terms_scales = pack4(terms)
    docs_words, docs_scales = pack4(docs)
    exact = 3.0 * (1.0 + 0.1 * np.random.standard_normal(T)) * t
    mass = np.random.standard_normal((B, T)) / np.sqrt(T) / t
    return {"terms_words": terms_words, "terms_scales": terms_scales,
            "docs_words": docs_words, "docs_scales": docs_scales,
            "exact": bf(exact), "mass": bf(mass)}


def reference(terms_words, terms_scales, docs_words, docs_scales, exact, mass):
    a = unpack4(terms_words, terms_scales)
    v = unpack4(docs_words, docs_scales)
    score = a.T @ v
    best = score.reshape(T, D, L).max(axis=2)
    cost = f64(exact)[:, None] - best
    return mxq(f64(mass), 1, "e4m3") @ mxq(cost, 0, "e4m3")

@@ -1,0 +1,265 @@
+from contextlib import ExitStack
+
+import concourse.mybir as mybir
+from concourse.masks import make_identity
+
+B, T, K, D, L = 1024, 1024, 1024, 512, 8
+FLOPS = 2 * K * T * D * L + 2 * B * T * D
+
+F32 = mybir.dt.float32
+BF16 = mybir.dt.bfloat16
+I32 = mybir.dt.int32
+U32 = mybir.dt.uint32
+U16 = mybir.dt.uint16
+U8 = mybir.dt.uint8
+FP8X4 = mybir.dt.float8_e4m3fn_x4
+FP4X4 = mybir.dt.float4_e2m1fn_x4
+ALU = mybir.AluOpType
+ACT = mybir.ActivationFunctionType
+
+P = 128
+PACK = 4
+K_PASS = P * PACK
+BANK = 512
+BANKS = 8
+DOCS = BANK // L
+HALF = L // 2
+E_PASSES = K // K_PASS
+T_PASSES = T // K_PASS
+B_TILES = B // P
+RUN = 4
+
+
+def tile_relaxed_word_mover_s4_kernel(tc, terms_words, terms_scales, docs_words, docs_scales, exact, mass, out):
+    nc = tc.nc
+    with ExitStack() as ctx:
+        keep = ctx.enter_context(tc.tile_pool(name="keep", bufs=1))
+        work = ctx.enter_context(tc.tile_pool(name="work", bufs=3))
+        psum = ctx.enter_context(tc.psum_pool(name="psum", bufs=1))
+        ctx.enter_context(tc.manual_schedule())
+
+        used = []
+
+        def next_bank():
+            n = len(used)
+            used.append(n)
+            return psum.tile([P, BANK], F32, name="bank_%d" % n, tag="bank%d" % (n % BANKS))
+
+        def load_words(src, name, col0, cols):
+            tile = keep.tile([P, E_PASSES, 2 * cols], U8, name=name, align_bytes=64)
+            view = src.bitcast(I32).rearrange("g p w -> p g w")
+            nc.sync.dma_start(out=tile[:].bitcast(I32), in_=view[:, :, col0 // 2 : (col0 + cols) // 2])
+            return tile
+
+        def zeroed_plane(name, cols):
+            tile = keep.tile([P, E_PASSES, cols], U8, name=name, align_bytes=64)
+            nc.vector.memset(tile[:].bitcast(I32), 0)
+            return tile
+
+        def load_scales(src, plane, col0, cols):
+            view = src.bitcast(I32).rearrange("g (q r) w -> r q g w", r=4)
+            for r in range(4):
+                nc.sync.dma_start(out=plane[r:P:32, :, :].bitcast(I32), in_=view[r, :, :, col0 // 4 : (col0 + cols) // 4])
+
+        def load_mass(h):
+            tile = keep.tile([P, RUN, T], BF16, name="mass_raw_%d" % h)
+            rows = mass[h * RUN * P : (h + 1) * RUN * P, :]
+            nc.sync.dma_start(out=tile[:], in_=rows.rearrange("(j p) k -> p j k", p=P))
+            return tile
+
+        EARLY = 2 * BANK
+        term_scales_raw = zeroed_plane("term_scales_raw", T)
+        doc_scales_early = zeroed_plane("doc_scales_early", EARLY)
+        doc_scales_late = zeroed_plane("doc_scales_late", D * L - EARLY)
+        load_scales(terms_scales, term_scales_raw, 0, T)
+        term_words_raw = [load_words(terms_words, "term_words_raw_0", 0, K_PASS)]
+        doc_words = [(load_words(docs_words, "doc_words_0", 0, BANK), 0)]
+        load_scales(docs_scales, doc_scales_early, 0, EARLY)
+        exact_sb = keep.tile([P, T_PASSES, PACK], BF16, name="exact_sb")
+        nc.sync.dma_start(out=exact_sb[:], in_=exact.rearrange("(g p t) -> p g t", p=P, t=PACK))
+        term_words_raw.append(load_words(terms_words, "term_words_raw_1", K_PASS, K_PASS))
+        doc_words.append((load_words(docs_words, "doc_words_1", BANK, BANK), 0))
+        load_scales(docs_scales, doc_scales_late, EARLY, D * L - EARLY)
+        mass_raw = [load_mass(0)]
+        tile23 = load_words(docs_words, "doc_words_23", 2 * BANK, 2 * BANK)
+        doc_words.extend([(tile23, i) for i in range(2)])
+        mass_raw.append(load_mass(1))
+        tile47 = load_words(docs_words, "doc_words_47", 4 * BANK, 4 * BANK)
+        doc_words.extend([(tile47, i) for i in range(4)])
+
+        ident = keep.tile([P, P], F32, name="ident")
+        make_identity(nc, ident[:])
+
+        neg_exact = keep.tile([P, T_PASSES, PACK], F32, name="neg_exact")
+        nc.scalar.activation(out=neg_exact[:], in_=exact_sb[:], func=ACT.Copy, scale=-1.0)
+
+        term_words = {}
+        term_scales = {}
+
+        def deal(g, t):
+            words = keep.tile([P, E_PASSES, 2 * P], U8, name="term_words_%d_%d" % (g, t), align_bytes=64)
+            scales = keep.tile([P, E_PASSES, P], U8, name="term_scales_%d_%d" % (g, t), align_bytes=64)
+            nc.vector.tensor_copy(out=scales[:], in_=term_scales_raw[:, :, g * K_PASS + t : (g + 1) * K_PASS : PACK])
+            nc.vector.tensor_copy(out=words[:].bitcast(U16), in_=term_words_raw[g][:].bitcast(U16)[:, :, t:K_PASS:PACK])
+            term_words[g, t] = words
+            term_scales[g, t] = scales
+
+        ranges = [(0, 256), (256, 128), (384, 128)]
+        cost_codes = {}
+        cost_scales = {}
+        for n, (d0, width) in enumerate(ranges):
+            for g in range(T_PASSES):
+                cost_codes[n, g] = keep.tile([P, width], U32, name="cost_codes_%d_%d" % (n, g), align_bytes=64)
+                cost_scales[n, g] = keep.tile([P, width], U8, name="cost_scales_%d_%d" % (n, g), align_bytes=64)
+        mass_codes = {}
+        mass_scales = {}
+
+        finishing = []
+        quantising = []
+
+        def run_deferred():
+            if finishing:
+                finishing.pop(0)()
+            if quantising:
+                quantising.pop(0)()
+
+        def score_quad(c, g, beside):
+            top4 = work.tile([P, PACK, HALF * DOCS], BF16, name="top4")
+            for t in range(PACK):
+                bank = next_bank()
+                words, slot = doc_words[c]
+                plane, col0 = (doc_scales_early, c * BANK) if c * BANK < EARLY else (doc_scales_late, c * BANK - EARLY)
+                for e in range(E_PASSES):
+                    nc.tensor.matmul_mx(
+                        out=bank[:],
+                        lhsT=term_words[g, t][:, e, :].bitcast(FP4X4),
+                        lhsT_scale=term_scales[g, t][:, e, :],
+                        rhs=words[:, e, slot * 2 * BANK : (slot + 1) * 2 * BANK].bitcast(FP4X4),
+                        rhs_scale=plane[:, e, col0 : col0 + BANK],
+                        start=(e == 0),
+                        stop=(e == E_PASSES - 1),
+                    )
+                by_word = bank[:].rearrange("p (d l) -> p l d", l=L)
+                low = work.tile([P, HALF, DOCS], BF16, name="low", bufs=6)
+                bias = neg_exact[:, g, t : t + 1]
+                nc.scalar.activation(out=low[:], in_=by_word[:, :HALF, :], func=ACT.Identity, bias=bias, scale=1.0)
+                nc.vector.scalar_tensor_tensor(
+                    out=top4[:, t, :].rearrange("p (l d) -> p l d", l=HALF),
+                    in0=by_word[:, HALF:, :],
+                    scalar=bias,
+                    in1=low[:],
+                    op0=ALU.add,
+                    op1=ALU.max,
+                )
+                run_deferred()
+                if beside:
+                    beside(t)
+
+            top2 = work.tile([P, PACK, 2 * DOCS], BF16, name="top2")
+            best = work.tile([P, DOCS * PACK], BF16, name="best", align_bytes=64)
+            n = [i for i, (d0, width) in enumerate(ranges) if d0 <= c * DOCS < d0 + width][0]
+            col = c * DOCS - ranges[n][0]
+
+            def halve():
+                nc.vector.tensor_tensor(out=top2[:], in0=top4[:, :, : 2 * DOCS], in1=top4[:, :, 2 * DOCS :], op=ALU.max)
+
+            def interleave():
+                nc.vector.tensor_tensor(
+                    out=best[:].rearrange("p (c i t) -> p c t i", i=4, t=PACK),
+                    in0=top2[:, :, :DOCS].rearrange("p t (c i) -> p c t i", i=4),
+                    in1=top2[:, :, DOCS:].rearrange("p t (c i) -> p c t i", i=4),
+                    op=ALU.max,
+                )
+
+            def quantise():
+                nc.vector.quantize_mx(
+                    out=cost_codes[n, g][:, col : col + DOCS].bitcast(FP8X4),
+                    scales=cost_scales[n, g][:, col : col + DOCS],
+                    in_=best[:],
+                )
+
+            finishing.extend([halve, interleave, quantise])
+
+        def mass_run(h):
+            for j in range(h * RUN, (h + 1) * RUN):
+                bank = next_bank()
+                pairs = mass_raw[h][:, j - h * RUN, :].bitcast(F32)
+                for g in range(T_PASSES):
+                    for u in range(2):
+                        q = 2 * g + u
+                        nc.tensor.transpose(bank[:, q * P : (q + 1) * P], pairs[:, 256 * g + u : 256 * (g + 1) : 2], ident[:])
+                grouped = work.tile([P, T], BF16, name="grouped", align_bytes=64)
+                nc.scalar.copy(
+                    out=grouped[:].bitcast(F32).rearrange("p (g b u) -> p g b u", g=T_PASSES, u=2),
+                    in_=bank[:].rearrange("p (g u b) -> p g b u", g=T_PASSES, u=2),
+                )
+                run_deferred()
+                mass_codes[j] = keep.tile([P, T_PASSES * P], U32, name="mass_codes_%d" % j, align_bytes=64)
+                mass_scales[j] = keep.tile([P, T_PASSES * P], U8, name="mass_scales_%d" % j, align_bytes=64)
+                quantising.append(
+                    lambda j=j, grouped=grouped: nc.vector.quantize_mx(
+                        out=mass_codes[j][:].bitcast(FP8X4), scales=mass_scales[j][:], in_=grouped[:]
+                    )
+                )
+
+        def weigh(dst, n, j, g):
+            nc.tensor.matmul_mx(
+                out=dst,
+                lhsT=mass_codes[j][:, g * P : (g + 1) * P].bitcast(FP8X4),
+                lhsT_scale=mass_scales[j][:, g * P : (g + 1) * P],
+                rhs=cost_codes[n, g][:].bitcast(FP8X4),
+                rhs_scale=cost_scales[n, g][:],
+                start=(g == 0),
+                stop=(g == T_PASSES - 1),
+            )
+
+        out_view = out.rearrange("(j p) d -> p j d", p=P)
+
+        def output_range(n):
+            d0, width = ranges[n]
+            per_bank = BANK // width
+            for j0 in range(0, B_TILES, per_bank):
+                bank = next_bank()
+                for i in range(per_bank):
+                    for g in range(T_PASSES):
+                        weigh(bank[:, i * width : (i + 1) * width], n, j0 + i, g)
+                result = work.tile([P, BANK], F32, name="result", bufs=4)
+                nc.scalar.activation(out=result[:], in_=bank[:], func=ACT.Copy, scale=-1.0)
+                nc.sync.dma_start(
+                    out=out_view[:, j0 : j0 + per_bank, d0 : d0 + width],
+                    in_=result[:].rearrange("p (i d) -> p i d", d=width),
+                )
+                run_deferred()
+
+        def last_range(n):
+            d0, width = ranges[n]
+            banks = [next_bank() for j in range(B_TILES)]
+            for j in range(B_TILES):
+                weigh(banks[j][:, :width], n, j, 0)
+            while finishing:
+                run_deferred()
+            result = keep.tile([P, B_TILES, width], F32, name="last_result")
+            for j in range(B_TILES):
+                weigh(banks[j][:, :width], n, j, 1)
+                if j % 2 == 0:
+                    nc.scalar.activation(out=result[:, j, :], in_=banks[j][:, :width], func=ACT.Copy, scale=-1.0)
+                else:
+                    nc.vector.tensor_scalar(
+                        out=result[:, j, :], in0=banks[j][:, :width], scalar1=-1.0, scalar2=None, op0=ALU.mult
+                    )
+                    nc.sync.dma_start(out=out_view[:, j - 1 : j + 1, d0 : d0 + width], in_=result[:, j - 1 : j + 1, :])
+
+        for t in range(PACK):
+            deal(0, t)
+        quads = [(2 * pair + i, g) for pair in range(D // DOCS // 2) for g in range(T_PASSES) for i in range(2)]
+        for q, (c, g) in enumerate(quads):
+            score_quad(c, g, (lambda t: deal(1, t)) if q == 0 else None)
+            if q == 3:
+                mass_run(0)
+            if q == 5:
+                mass_run(1)
+            if q == 9:
+                output_range(0)
+            if q == 13:
+                output_range(1)
+        last_range(2)

@@ -123,8 +123,15 @@ def tile_relaxed_word_mover_s4_kernel(tc, terms_words, terms_scales, docs_words,
             if quantising:
                 quantising.pop(0)()
 
-        def score_quad(c, g, beside):
+        def score_quad(c, g, beside, last):
             top4 = work.tile([P, PACK, HALF * DOCS], BF16, name="top4")
+            top2 = work.tile([P, PACK, 2 * DOCS], BF16, name="top2")
+
+            def halve(t0, t1):
+                nc.vector.tensor_tensor(
+                    out=top2[:, t0:t1, :], in0=top4[:, t0:t1, : 2 * DOCS], in1=top4[:, t0:t1, 2 * DOCS :], op=ALU.max
+                )
+
             for t in range(PACK):
                 bank = next_bank()
                 words, slot = doc_words[c]
@@ -152,16 +159,13 @@ def tile_relaxed_word_mover_s4_kernel(tc, terms_words, terms_scales, docs_words,
                     op1=ALU.max,
                 )
                 run_deferred()
-                if beside:
-                    beside(t)
+                beside(t)
+                if last and t == PACK - 2:
+                    halve(0, PACK - 1)
 
-            top2 = work.tile([P, PACK, 2 * DOCS], BF16, name="top2")
             best = work.tile([P, DOCS * PACK], BF16, name="best", align_bytes=64)
             n = [i for i, (d0, width) in enumerate(ranges) if d0 <= c * DOCS < d0 + width][0]
             col = c * DOCS - ranges[n][0]
-
-            def halve():
-                nc.vector.tensor_tensor(out=top2[:], in0=top4[:, :, : 2 * DOCS], in1=top4[:, :, 2 * DOCS :], op=ALU.max)
 
             def interleave():
                 nc.vector.tensor_tensor(
@@ -178,16 +182,25 @@ def tile_relaxed_word_mover_s4_kernel(tc, terms_words, terms_scales, docs_words,
                     in_=best[:],
                 )
 
-            finishing.extend([halve, interleave, quantise])
+            finishing.extend([lambda: halve(PACK - 1 if last else 0, PACK), interleave, quantise])
+
+        mass_sorted = {}
+
+        def sort_mass(j):
+            pairs = mass_raw[j // RUN][:, j % RUN, :].bitcast(F32)
+            tile = keep.tile([P, T // 2], F32, name="mass_sorted_%d" % j, align_bytes=64)
+            nc.scalar.copy(
+                out=tile[:].rearrange("p (g u m) -> p g u m", g=T_PASSES, u=2),
+                in_=pairs.rearrange("p (g m u) -> p g u m", g=T_PASSES, u=2),
+            )
+            mass_sorted[j] = tile
 
         def mass_run(h):
             for j in range(h * RUN, (h + 1) * RUN):
                 bank = next_bank()
-                pairs = mass_raw[h][:, j - h * RUN, :].bitcast(F32)
-                for g in range(T_PASSES):
-                    for u in range(2):
-                        q = 2 * g + u
-                        nc.tensor.transpose(bank[:, q * P : (q + 1) * P], pairs[:, 256 * g + u : 256 * (g + 1) : 2], ident[:])
+                for q in range(2 * T_PASSES):
+                    cols = slice(q * P, (q + 1) * P)
+                    nc.tensor.transpose(bank[:, cols], mass_sorted[j][:, cols], ident[:])
                 grouped = work.tile([P, T], BF16, name="grouped", align_bytes=64)
                 nc.scalar.copy(
                     out=grouped[:].bitcast(F32).rearrange("p (g b u) -> p g b u", g=T_PASSES, u=2),
@@ -252,14 +265,24 @@ def tile_relaxed_word_mover_s4_kernel(tc, terms_words, terms_scales, docs_words,
         for t in range(PACK):
             deal(0, t)
         quads = [(2 * pair + i, g) for pair in range(D // DOCS // 2) for g in range(T_PASSES) for i in range(2)]
+        FIRST_SORT = 3
+
+        def beside_quad(q):
+            def beside(t):
+                if q == 0:
+                    deal(1, t)
+                if t == 0 and FIRST_SORT <= q < FIRST_SORT + B_TILES:
+                    sort_mass(q - FIRST_SORT)
+
+            return beside
+
         for q, (c, g) in enumerate(quads):
-            score_quad(c, g, (lambda t: deal(1, t)) if q == 0 else None)
-            if q == 3:
+            score_quad(c, g, beside_quad(q), q == len(quads) - 1)
+            if q == FIRST_SORT + RUN - 1:
                 mass_run(0)
-            if q == 5:
+            if q == FIRST_SORT + 2 * RUN - 1:
                 mass_run(1)
-            if q == 9:
+            if q == FIRST_SORT + 2 * RUN:
                 output_range(0)
-            if q == 13:
-                output_range(1)
+        output_range(1)
         last_range(2)

@@ -123,15 +123,8 @@ def tile_relaxed_word_mover_s4_kernel(tc, terms_words, terms_scales, docs_words,
             if quantising:
                 quantising.pop(0)()
 
-        def score_quad(c, g, beside, last):
+        def score_quad(c, g, beside):
             top4 = work.tile([P, PACK, HALF * DOCS], BF16, name="top4")
-            top2 = work.tile([P, PACK, 2 * DOCS], BF16, name="top2")
-
-            def halve(t0, t1):
-                nc.vector.tensor_tensor(
-                    out=top2[:, t0:t1, :], in0=top4[:, t0:t1, : 2 * DOCS], in1=top4[:, t0:t1, 2 * DOCS :], op=ALU.max
-                )
-
             for t in range(PACK):
                 bank = next_bank()
                 words, slot = doc_words[c]
@@ -160,19 +153,19 @@ def tile_relaxed_word_mover_s4_kernel(tc, terms_words, terms_scales, docs_words,
                 )
                 run_deferred()
                 beside(t)
-                if last and t == PACK - 2:
-                    halve(0, PACK - 1)
 
+            top2 = work.tile([P, PACK, 2 * DOCS], BF16, name="top2")
+            top1 = work.tile([P, PACK, DOCS], BF16, name="top1")
             best = work.tile([P, DOCS * PACK], BF16, name="best", align_bytes=64)
             n = [i for i, (d0, width) in enumerate(ranges) if d0 <= c * DOCS < d0 + width][0]
             col = c * DOCS - ranges[n][0]
 
+            def halve(dst, src, width):
+                nc.vector.tensor_tensor(out=dst[:], in0=src[:, :, :width], in1=src[:, :, width:], op=ALU.max)
+
             def interleave():
-                nc.vector.tensor_tensor(
-                    out=best[:].rearrange("p (c i t) -> p c t i", i=4, t=PACK),
-                    in0=top2[:, :, :DOCS].rearrange("p t (c i) -> p c t i", i=4),
-                    in1=top2[:, :, DOCS:].rearrange("p t (c i) -> p c t i", i=4),
-                    op=ALU.max,
+                nc.vector.tensor_copy(
+                    out=best[:].rearrange("p (d t) -> p d t", t=PACK), in_=top1[:].rearrange("p t d -> p d t")
                 )
 
             def quantise():
@@ -182,7 +175,7 @@ def tile_relaxed_word_mover_s4_kernel(tc, terms_words, terms_scales, docs_words,
                     in_=best[:],
                 )
 
-            finishing.extend([lambda: halve(PACK - 1 if last else 0, PACK), interleave, quantise])
+            finishing.extend([lambda: halve(top2, top4, 2 * DOCS), lambda: halve(top1, top2, DOCS), interleave, quantise])
 
         mass_sorted = {}
 
@@ -228,10 +221,10 @@ def tile_relaxed_word_mover_s4_kernel(tc, terms_words, terms_scales, docs_words,
 
         out_view = out.rearrange("(j p) d -> p j d", p=P)
 
-        def output_range(n):
+        def output_range(n, first, last):
             d0, width = ranges[n]
             per_bank = BANK // width
-            for j0 in range(0, B_TILES, per_bank):
+            for j0 in range(first, last, per_bank):
                 bank = next_bank()
                 for i in range(per_bank):
                     for g in range(T_PASSES):
@@ -277,12 +270,13 @@ def tile_relaxed_word_mover_s4_kernel(tc, terms_words, terms_scales, docs_words,
             return beside
 
         for q, (c, g) in enumerate(quads):
-            score_quad(c, g, beside_quad(q), q == len(quads) - 1)
+            score_quad(c, g, beside_quad(q))
             if q == FIRST_SORT + RUN - 1:
                 mass_run(0)
             if q == FIRST_SORT + 2 * RUN - 1:
                 mass_run(1)
             if q == FIRST_SORT + 2 * RUN:
-                output_range(0)
-        output_range(1)
+                output_range(0, 0, B_TILES - 2)
+        output_range(0, B_TILES - 2, B_TILES)
+        output_range(1, 0, B_TILES)
         last_range(2)

from contextlib import ExitStack

import concourse.mybir as mybir
from concourse.masks import make_identity

B, T, K, D, L = 1024, 1024, 1024, 512, 8
FLOPS = 2 * K * T * D * L + 2 * B * T * D

F32 = mybir.dt.float32
BF16 = mybir.dt.bfloat16
I32 = mybir.dt.int32
U32 = mybir.dt.uint32
U16 = mybir.dt.uint16
U8 = mybir.dt.uint8
FP8X4 = mybir.dt.float8_e4m3fn_x4
FP4X4 = mybir.dt.float4_e2m1fn_x4
ALU = mybir.AluOpType
ACT = mybir.ActivationFunctionType

P = 128
PACK = 4
K_PASS = P * PACK
BANK = 512
BANKS = 8
DOCS = BANK // L
HALF = L // 2
E_PASSES = K // K_PASS
T_PASSES = T // K_PASS
B_TILES = B // P
RUN = 4


def tile_relaxed_word_mover_s4_kernel(tc, terms_words, terms_scales, docs_words, docs_scales, exact, mass, out):
    nc = tc.nc
    with ExitStack() as ctx:
        keep = ctx.enter_context(tc.tile_pool(name="keep", bufs=1))
        work = ctx.enter_context(tc.tile_pool(name="work", bufs=3))
        psum = ctx.enter_context(tc.psum_pool(name="psum", bufs=1))
        ctx.enter_context(tc.manual_schedule())

        used = []

        def next_bank():
            n = len(used)
            used.append(n)
            return psum.tile([P, BANK], F32, name="bank_%d" % n, tag="bank%d" % (n % BANKS))

        def load_words(src, name, col0, cols):
            tile = keep.tile([P, E_PASSES, 2 * cols], U8, name=name, align_bytes=64)
            view = src.bitcast(I32).rearrange("g p w -> p g w")
            nc.sync.dma_start(out=tile[:].bitcast(I32), in_=view[:, :, col0 // 2 : (col0 + cols) // 2])
            return tile

        def zeroed_plane(name, cols):
            tile = keep.tile([P, E_PASSES, cols], U8, name=name, align_bytes=64)
            nc.vector.memset(tile[:].bitcast(I32), 0)
            return tile

        def load_scales(src, plane, col0, cols):
            view = src.bitcast(I32).rearrange("g (q r) w -> r q g w", r=4)
            for r in range(4):
                nc.sync.dma_start(out=plane[r:P:32, :, :].bitcast(I32), in_=view[r, :, :, col0 // 4 : (col0 + cols) // 4])

        def load_mass(h):
            tile = keep.tile([P, RUN, T], BF16, name="mass_raw_%d" % h)
            rows = mass[h * RUN * P : (h + 1) * RUN * P, :]
            nc.sync.dma_start(out=tile[:], in_=rows.rearrange("(j p) k -> p j k", p=P))
            return tile

        EARLY = 2 * BANK
        term_scales_raw = zeroed_plane("term_scales_raw", T)
        doc_scales_early = zeroed_plane("doc_scales_early", EARLY)
        doc_scales_late = zeroed_plane("doc_scales_late", D * L - EARLY)
        load_scales(terms_scales, term_scales_raw, 0, T)
        term_words_raw = [load_words(terms_words, "term_words_raw_0", 0, K_PASS)]
        doc_words = [(load_words(docs_words, "doc_words_0", 0, BANK), 0)]
        load_scales(docs_scales, doc_scales_early, 0, EARLY)
        exact_sb = keep.tile([P, T_PASSES, PACK], BF16, name="exact_sb")
        nc.sync.dma_start(out=exact_sb[:], in_=exact.rearrange("(g p t) -> p g t", p=P, t=PACK))
        term_words_raw.append(load_words(terms_words, "term_words_raw_1", K_PASS, K_PASS))
        doc_words.append((load_words(docs_words, "doc_words_1", BANK, BANK), 0))
        load_scales(docs_scales, doc_scales_late, EARLY, D * L - EARLY)
        mass_raw = [load_mass(0)]
        tile23 = load_words(docs_words, "doc_words_23", 2 * BANK, 2 * BANK)
        doc_words.extend([(tile23, i) for i in range(2)])
        mass_raw.append(load_mass(1))
        tile47 = load_words(docs_words, "doc_words_47", 4 * BANK, 4 * BANK)
        doc_words.extend([(tile47, i) for i in range(4)])

        ident = keep.tile([P, P], F32, name="ident")
        make_identity(nc, ident[:])

        neg_exact = keep.tile([P, T_PASSES, PACK], F32, name="neg_exact")
        nc.scalar.activation(out=neg_exact[:], in_=exact_sb[:], func=ACT.Copy, scale=-1.0)

        term_words = {}
        term_scales = {}

        def deal(g, t):
            words = keep.tile([P, E_PASSES, 2 * P], U8, name="term_words_%d_%d" % (g, t), align_bytes=64)
            scales = keep.tile([P, E_PASSES, P], U8, name="term_scales_%d_%d" % (g, t), align_bytes=64)
            nc.vector.tensor_copy(out=scales[:], in_=term_scales_raw[:, :, g * K_PASS + t : (g + 1) * K_PASS : PACK])
            nc.vector.tensor_copy(out=words[:].bitcast(U16), in_=term_words_raw[g][:].bitcast(U16)[:, :, t:K_PASS:PACK])
            term_words[g, t] = words
            term_scales[g, t] = scales

        ranges = [(0, 256), (256, 128), (384, 128)]
        cost_codes = {}
        cost_scales = {}
        for n, (d0, width) in enumerate(ranges):
            for g in range(T_PASSES):
                cost_codes[n, g] = keep.tile([P, width], U32, name="cost_codes_%d_%d" % (n, g), align_bytes=64)
                cost_scales[n, g] = keep.tile([P, width], U8, name="cost_scales_%d_%d" % (n, g), align_bytes=64)
        mass_codes = {}
        mass_scales = {}

        finishing = []
        quantising = []

        def run_deferred():
            if finishing:
                finishing.pop(0)()
            if quantising:
                quantising.pop(0)()

        def score_quad(c, g, beside):
            top4 = work.tile([P, PACK, HALF * DOCS], BF16, name="top4")
            for t in range(PACK):
                bank = next_bank()
                words, slot = doc_words[c]
                plane, col0 = (doc_scales_early, c * BANK) if c * BANK < EARLY else (doc_scales_late, c * BANK - EARLY)
                for e in range(E_PASSES):
                    nc.tensor.matmul_mx(
                        out=bank[:],
                        lhsT=term_words[g, t][:, e, :].bitcast(FP4X4),
                        lhsT_scale=term_scales[g, t][:, e, :],
                        rhs=words[:, e, slot * 2 * BANK : (slot + 1) * 2 * BANK].bitcast(FP4X4),
                        rhs_scale=plane[:, e, col0 : col0 + BANK],
                        start=(e == 0),
                        stop=(e == E_PASSES - 1),
                    )
                by_word = bank[:].rearrange("p (d l) -> p l d", l=L)
                low = work.tile([P, HALF, DOCS], BF16, name="low", bufs=6)
                bias = neg_exact[:, g, t : t + 1]
                nc.scalar.activation(out=low[:], in_=by_word[:, :HALF, :], func=ACT.Identity, bias=bias, scale=1.0)
                nc.vector.scalar_tensor_tensor(
                    out=top4[:, t, :].rearrange("p (l d) -> p l d", l=HALF),
                    in0=by_word[:, HALF:, :],
                    scalar=bias,
                    in1=low[:],
                    op0=ALU.add,
                    op1=ALU.max,
                )
                run_deferred()
                beside(t)

            top2 = work.tile([P, PACK, 2 * DOCS], BF16, name="top2")
            top1 = work.tile([P, PACK, DOCS], BF16, name="top1")
            best = work.tile([P, DOCS * PACK], BF16, name="best", align_bytes=64)
            n = [i for i, (d0, width) in enumerate(ranges) if d0 <= c * DOCS < d0 + width][0]
            col = c * DOCS - ranges[n][0]

            def halve(dst, src, width):
                nc.vector.tensor_tensor(out=dst[:], in0=src[:, :, :width], in1=src[:, :, width:], op=ALU.max)

            def interleave():
                nc.vector.tensor_copy(
                    out=best[:].rearrange("p (d t) -> p d t", t=PACK), in_=top1[:].rearrange("p t d -> p d t")
                )

            def quantise():
                nc.vector.quantize_mx(
                    out=cost_codes[n, g][:, col : col + DOCS].bitcast(FP8X4),
                    scales=cost_scales[n, g][:, col : col + DOCS],
                    in_=best[:],
                )

            finishing.extend([lambda: halve(top2, top4, 2 * DOCS), lambda: halve(top1, top2, DOCS), interleave, quantise])

        mass_sorted = {}

        def sort_mass(j):
            pairs = mass_raw[j // RUN][:, j % RUN, :].bitcast(F32)
            tile = keep.tile([P, T // 2], F32, name="mass_sorted_%d" % j, align_bytes=64)
            nc.scalar.copy(
                out=tile[:].rearrange("p (g u m) -> p g u m", g=T_PASSES, u=2),
                in_=pairs.rearrange("p (g m u) -> p g u m", g=T_PASSES, u=2),
            )
            mass_sorted[j] = tile

        def mass_run(h):
            for j in range(h * RUN, (h + 1) * RUN):
                bank = next_bank()
                for q in range(2 * T_PASSES):
                    cols = slice(q * P, (q + 1) * P)
                    nc.tensor.transpose(bank[:, cols], mass_sorted[j][:, cols], ident[:])
                grouped = work.tile([P, T], BF16, name="grouped", align_bytes=64)
                nc.scalar.copy(
                    out=grouped[:].bitcast(F32).rearrange("p (g b u) -> p g b u", g=T_PASSES, u=2),
                    in_=bank[:].rearrange("p (g u b) -> p g b u", g=T_PASSES, u=2),
                )
                run_deferred()
                mass_codes[j] = keep.tile([P, T_PASSES * P], U32, name="mass_codes_%d" % j, align_bytes=64)
                mass_scales[j] = keep.tile([P, T_PASSES * P], U8, name="mass_scales_%d" % j, align_bytes=64)
                quantising.append(
                    lambda j=j, grouped=grouped: nc.vector.quantize_mx(
                        out=mass_codes[j][:].bitcast(FP8X4), scales=mass_scales[j][:], in_=grouped[:]
                    )
                )

        def weigh(dst, n, j, g):
            nc.tensor.matmul_mx(
                out=dst,
                lhsT=mass_codes[j][:, g * P : (g + 1) * P].bitcast(FP8X4),
                lhsT_scale=mass_scales[j][:, g * P : (g + 1) * P],
                rhs=cost_codes[n, g][:].bitcast(FP8X4),
                rhs_scale=cost_scales[n, g][:],
                start=(g == 0),
                stop=(g == T_PASSES - 1),
            )

        out_view = out.rearrange("(j p) d -> p j d", p=P)

        def output_range(n, first, last):
            d0, width = ranges[n]
            per_bank = BANK // width
            for j0 in range(first, last, per_bank):
                bank = next_bank()
                for i in range(per_bank):
                    for g in range(T_PASSES):
                        weigh(bank[:, i * width : (i + 1) * width], n, j0 + i, g)
                result = work.tile([P, BANK], F32, name="result", bufs=4)
                nc.scalar.activation(out=result[:], in_=bank[:], func=ACT.Copy, scale=-1.0)
                nc.sync.dma_start(
                    out=out_view[:, j0 : j0 + per_bank, d0 : d0 + width],
                    in_=result[:].rearrange("p (i d) -> p i d", d=width),
                )
                run_deferred()

        def last_range(n):
            d0, width = ranges[n]
            banks = [next_bank() for j in range(B_TILES)]
            for j in range(B_TILES):
                weigh(banks[j][:, :width], n, j, 0)
            while finishing:
                run_deferred()
            result = keep.tile([P, B_TILES, width], F32, name="last_result")
            for j in range(B_TILES):
                weigh(banks[j][:, :width], n, j, 1)
                if j % 2 == 0:
                    nc.scalar.activation(out=result[:, j, :], in_=banks[j][:, :width], func=ACT.Copy, scale=-1.0)
                else:
                    nc.vector.tensor_scalar(
                        out=result[:, j, :], in0=banks[j][:, :width], scalar1=-1.0, scalar2=None, op0=ALU.mult
                    )
                    nc.sync.dma_start(out=out_view[:, j - 1 : j + 1, d0 : d0 + width], in_=result[:, j - 1 : j + 1, :])

        for t in range(PACK):
            deal(0, t)
        quads = [(2 * pair + i, g) for pair in range(D // DOCS // 2) for g in range(T_PASSES) for i in range(2)]
        FIRST_SORT = 3

        def beside_quad(q):
            def beside(t):
                if q == 0:
                    deal(1, t)
                if t == 0 and FIRST_SORT <= q < FIRST_SORT + B_TILES:
                    sort_mass(q - FIRST_SORT)

            return beside

        for q, (c, g) in enumerate(quads):
            score_quad(c, g, beside_quad(q))
            if q == FIRST_SORT + RUN - 1:
                mass_run(0)
            if q == FIRST_SORT + 2 * RUN - 1:
                mass_run(1)
            if q == FIRST_SORT + 2 * RUN:
                output_range(0, 0, B_TILES - 2)
        output_range(0, B_TILES - 2, B_TILES)
        output_range(1, 0, B_TILES)
        last_range(2)
